import numpy as np
import ml_dtypes


def mxq(x, axis, fmt="e4m3"):
    dtype, down = {"e4m3": (ml_dtypes.float8_e4m3fn, 7), "e5m2": (ml_dtypes.float8_e5m2, 14)}[fmt]
    v = np.moveaxis(np.asarray(x, np.float32).astype(ml_dtypes.bfloat16).astype(np.float64), axis, -1)
    blocks = v.reshape(v.shape[:-1] + (-1, 32))
    amax = np.abs(blocks).max(-1, keepdims=True)
    byte = np.maximum(np.where(amax > 0, np.frexp(amax)[1] - 1 + 127, 0) - down, 1)
    scale = np.exp2(byte - 127.0)
    codes = (blocks / scale).astype(np.float32).astype(dtype).astype(np.float64)
    return np.moveaxis((codes * scale).reshape(v.shape), -1, axis)


WIDE = False


def mx_kscale(k):
    if not WIDE:
        return np.ones(k)
    levels = np.array([30, -30])
    if k % 512:
        return np.exp2(np.random.permutation(np.resize(levels, k // 32))).repeat(32)
    a = np.empty((k // 512, 16))
    for p in range(k // 512):
        a[p, :8] = np.random.permutation(np.resize(levels, 8))
        for g in range(8):
            far = levels[np.abs(levels - a[p, g]) >= 10]
            a[p, g + 8] = far[np.random.randint(len(far))]
    return np.exp2(a.ravel()).repeat(32)


def f64(x):
    return np.asarray(x).astype(np.float64)


def striped(idx):
    return np.tile(np.asarray(idx).reshape(-1, 16).T, (8, 1)).astype(np.uint16)


def unstriped(offs):
    return offs[:16].T.reshape(-1).astype(np.int64)


E2M1 = np.array([0.0, 0.5, 1.0, 1.5, 2.0, 3.0, 4.0, 6.0, -0.0, -0.5, -1.0, -1.5, -2.0, -3.0, -4.0, -6.0])


def pack_weight(w, fmt):
    k, n = w.shape
    w = f64(np.asarray(w, np.float32).astype(ml_dtypes.bfloat16)).reshape(k // 32, 32, n)
    amax = np.abs(w).max(1)
    if fmt in ("e4m3", "e5m2"):
        byte = np.frexp(amax)[1] - 1 + 127 - (7 if fmt == "e4m3" else 14)
    else:
        mant, ex = np.frexp(amax / 6.0)
        byte = np.where(mant > 0.5, ex, ex - 1) + 127
    byte = np.clip(np.where(amax > 0, byte, 1), 1, 254)
    scaled = (w * np.exp2(127.0 - byte)[:, None, :]).reshape(k, n).astype(np.float32)
    by_word = np.ascontiguousarray(scaled.reshape(k // 512, 128, 4, n).transpose(0, 1, 3, 2))
    if fmt in ("e4m3", "e5m2"):
        words = by_word.astype(ml_dtypes.float8_e4m3fn if fmt == "e4m3" else ml_dtypes.float8_e5m2).view(np.uint8)
    else:
        c = by_word.astype(ml_dtypes.float4_e2m1fn).view(np.uint8) & 0xF
        words = (c[..., 0::2] | (c[..., 1::2] << 4)).reshape(k // 512, 128, 2 * n)
    return np.ascontiguousarray(words), np.ascontiguousarray(byte.astype(np.uint8).reshape(k // 512, 16, n))


def unpack_weight(words, scales, fmt):
    g, _, n = scales.shape
    words = np.ascontiguousarray(words).reshape(g, 128, n, -1)
    if fmt in ("e4m3", "e5m2"):
        vals = words.view(ml_dtypes.float8_e4m3fn if fmt == "e4m3" else ml_dtypes.float8_e5m2).astype(np.float64)
    else:
        nib = np.empty((g, 128, n, 4), np.uint8)
        nib[..., 0::2] = words & 0xF
        nib[..., 1::2] = words >> 4
        vals = E2M1[nib]
    vals = vals * np.repeat(np.exp2(scales.astype(np.float64) - 127.0), 8, axis=1)[..., None]
    return vals.transpose(0, 1, 3, 2).reshape(g * 512, n)


def sgn(shape):
    return np.random.uniform(0.5, 2.0, shape) * np.where(np.random.standard_normal(shape) < 0, -1.0, 1.0)


K, T, J, F, Z, Q, O, R, N = 512, 1024, 256, 512, 1024, 128, 128, 512, 256


def setup_inputs():
    n = np.random.standard_normal
    idx = np.random.permutation(T)[:J]
    idx2 = np.random.permutation(Z)[:J]
    idx3 = np.random.permutation(J)[:O]
    idx4 = np.random.permutation(J)[:O]
    idx5 = np.random.permutation(J)[:O]
    idx6 = np.random.permutation(J)[:O]
    fk = mx_kscale(K)
    ff = mx_kscale(F)
    fr = mx_kscale(R)
    xtp = pack_weight(n((K, T)) / fk[:, None], "e5m2")
    xop = pack_weight(n((F, Z)) / ff[:, None], "e4m3")
    wp = pack_weight(n((K, Q)) * 1 / np.sqrt(K) * fk[:, None], "e2m1")
    w2p = pack_weight(n((K, Q)) * 1 / np.sqrt(K) * fk[:, None], "e2m1")
    w3p = pack_weight(n((F, Q)) * 1 / np.sqrt(F) * ff[:, None], "e4m3")
    w0p = pack_weight(n((F, Q)) * 1 / np.sqrt(F) * ff[:, None], "e2m1")
    wbp = pack_weight(n((R, N)) * 1 / np.sqrt(R) / fr[:, None], "e2m1")
    return {
        "xt_words": xtp[0],
        "xt_scales": xtp[1],
        "xo_words": xop[0],
        "xo_scales": xop[1],
        "w_words": wp[0],
        "w_scales": wp[1],
        "w2_words": w2p[0],
        "w2_scales": w2p[1],
        "w3_words": w3p[0],
        "w3_scales": w3p[1],
        "w0_words": w0p[0],
        "w0_scales": w0p[1],
        "sa": (np.random.uniform(0.5, 1.6, (Q, 1)) * fr[::4, None]).astype(np.float32),
        "sb": (sgn((Q, 1)) * fr[::4, None]).astype(np.float32),
        "sd": (np.random.uniform(0.5, 1.6, (Q, 1)) * fr[::4, None]).astype(np.float32),
        "se": (sgn((Q, 1)) * fr[::4, None]).astype(np.float32),
        "wb_words": wbp[0],
        "wb_scales": wbp[1],
        "offs": striped(idx),
        "offs2": striped(idx2),
        "offs3": striped(idx3),
        "offs4": striped(idx4),
        "offs5": striped(idx5),
        "offs6": striped(idx6),
    }


def reference(xt_words, xt_scales, xo_words, xo_scales, w_words, w_scales, w2_words, w2_scales, w3_words, w3_scales, w0_words, w0_scales, sa, sb, sd, se, wb_words, wb_scales, offs, offs2, offs3, offs4, offs5, offs6):
    idx = unstriped(offs)
    idx2 = unstriped(offs2)
    idx3 = unstriped(offs3)
    idx4 = unstriped(offs4)
    idx5 = unstriped(offs5)
    idx6 = unstriped(offs6)
    xtu = unpack_weight(xt_words, xt_scales, "e5m2")
    xou = unpack_weight(xo_words, xo_scales, "e4m3")
    wu = unpack_weight(w_words, w_scales, "e2m1")
    w2u = unpack_weight(w2_words, w2_scales, "e2m1")
    w3u = unpack_weight(w3_words, w3_scales, "e4m3")
    w0u = unpack_weight(w0_words, w0_scales, "e2m1")
    wbu = unpack_weight(wb_words, wb_scales, "e2m1")
    xtidxg = xtu[:, idx]
    a = wu.T @ xtidxg
    b = w2u.T @ xtidxg
    xoidx2g = xou[:, idx2]
    g = w3u.T @ xoidx2g
    d = w0u.T @ xoidx2g
    v0 = a[:, idx3] * f64(sa)
    v1 = g[:, idx4] * f64(sd)
    v2 = b[:, idx5] * f64(sb)
    v3 = d[:, idx6] * f64(se)
    hid = np.stack([v0, v1, v2, v3], axis=1).reshape(R, O)
    hidq = mxq(hid, 0, "e4m3")
    p = wbu.T @ hidq
    return p

@@ -1,0 +1,170 @@
+from contextlib import ExitStack
+
+import concourse.mybir as mybir
+
+F32 = mybir.dt.float32
+BF16 = mybir.dt.bfloat16
+I32 = mybir.dt.int32
+U32 = mybir.dt.uint32
+U16 = mybir.dt.uint16
+U8 = mybir.dt.uint8
+E4M3 = mybir.dt.float8_e4m3fn_x4
+E5M2 = mybir.dt.float8_e5m2_x4
+E2M1 = mybir.dt.float4_e2m1fn_x4
+COPY = mybir.ActivationFunctionType.Copy
+
+P = 128
+COLS = 1024
+SLOTS = 256
+FEATS = 128
+PLACES = 128
+OUTS = 256
+QUADS = 4
+ROWS = 4
+PACK = 4
+
+FLOPS = 2 * 512 * FEATS * SLOTS * 4 + 2 * 512 * OUTS * PLACES
+
+
+def tile_list_fourtowers_kernel(
+    tc, xt_words, xt_scales, xo_words, xo_scales, w_words, w_scales, w2_words, w2_scales,
+    w3_words, w3_scales, w0_words, w0_scales, sa, sb, sd, se, wb_words, wb_scales,
+    offs, offs2, offs3, offs4, offs5, offs6, out,
+):
+    nc = tc.nc
+    with ExitStack() as ctx:
+        pool = ctx.enter_context(tc.tile_pool(name="held", bufs=1))
+        psum = ctx.enter_context(tc.psum_pool(name="psum", bufs=1))
+
+        def sbuf(name, shape, dtype):
+            return pool.tile(shape, dtype, name=name, align_bytes=64)
+
+        def list_tile(name, src):
+            tile = sbuf(name, list(src.shape), U16)
+            nc.sync.dma_start(tile[:], src)
+            return tile
+
+        def fp8_words(src):
+            return src[0].rearrange("p c r -> p (c r)").bitcast(I32)
+
+        def by_quadrant(src):
+            return src[0].bitcast(I32).rearrange("(q r) n -> r q n", r=ROWS)
+
+        def spread(plane, stage):
+            for q in range(QUADS):
+                nc.vector.tensor_copy(plane[32 * q : 32 * q + ROWS, :].bitcast(I32), stage[0:ROWS, q, :])
+
+        xt_tab = sbuf("xt_tab", [P, COLS], I32)
+        xo_tab = sbuf("xo_tab", [P, COLS], I32)
+        xt_stage = sbuf("xt_stage", [ROWS, QUADS, COLS // 4], I32)
+        xo_stage = sbuf("xo_stage", [ROWS, QUADS, COLS // 4], I32)
+        xt_plane = sbuf("xt_plane", [P, COLS], U8)
+        xo_plane = sbuf("xo_plane", [P, COLS], U8)
+        w_stage = sbuf("w_stage", [ROWS, QUADS, FEATS], I32)
+        w_plane = sbuf("w_plane", [P, 4 * FEATS], U8)
+        wb_plane = sbuf("wb_plane", [P, OUTS], U8)
+        w_sb = sbuf("w_sb", [P, 2 * FEATS], U8)
+        w2_sb = sbuf("w2_sb", [P, 2 * FEATS], U8)
+        w3_sb = sbuf("w3_sb", [P, FEATS], I32)
+        w0_sb = sbuf("w0_sb", [P, 2 * FEATS], U8)
+        wb_sb = sbuf("wb_sb", [P, 2 * OUTS], U8)
+
+        for plane in (xt_plane, xo_plane, w_plane, wb_plane):
+            nc.vector.memset(plane[:].bitcast(I32), 0)
+
+        def stage_w(i, src):
+            nc.scalar.dma_start(w_stage[:, :, 32 * i : 32 * (i + 1)], by_quadrant(src))
+
+        nc.sync.dma_start(xt_tab[:], fp8_words(xt_words))
+        nc.scalar.dma_start(xt_stage[:], by_quadrant(xt_scales))
+        l_xt = list_tile("l_xt", offs)
+        nc.scalar.dma_start(xo_stage[:], by_quadrant(xo_scales))
+        nc.sync.dma_start(xo_tab[:], fp8_words(xo_words))
+        stage_w(0, w_scales)
+        l_xo = list_tile("l_xo", offs2)
+        stage_w(1, w2_scales)
+
+        factors = {}
+        for name, src in (("a", sa), ("b", sb), ("g", sd), ("d", se)):
+            factors[name] = sbuf("f_" + name, [P, 1], F32)
+            nc.gpsimd.dma_start(factors[name][:], src)
+        nc.gpsimd.dma_start(wb_sb[:].bitcast(I32), wb_words[0].bitcast(I32))
+
+        nc.scalar.dma_start(w_sb[:].bitcast(I32), w_words[0].bitcast(I32))
+        nc.sync.dma_start(w3_sb[:], fp8_words(w3_words))
+        nc.scalar.dma_start(w2_sb[:].bitcast(I32), w2_words[0].bitcast(I32))
+        nc.sync.dma_start(w0_sb[:].bitcast(I32), w0_words[0].bitcast(I32))
+        stage_w(2, w3_scales)
+        l_a = list_tile("l_a", offs3)
+        stage_w(3, w0_scales)
+        l_b = list_tile("l_b", offs5)
+        l_g = list_tile("l_g", offs4)
+        l_d = list_tile("l_d", offs6)
+        for q in range(QUADS):
+            nc.sync.dma_start(
+                wb_plane[32 * q : 32 * q + ROWS, :].bitcast(I32),
+                wb_scales[0, ROWS * q : ROWS * (q + 1), :].bitcast(I32),
+            )
+
+        xt_got = sbuf("xt_got", [P, SLOTS], U32)
+        xo_got = sbuf("xo_got", [P, SLOTS], U32)
+        xt_got_s = sbuf("xt_got_s", [P, SLOTS], U8)
+        xo_got_s = sbuf("xo_got_s", [P, SLOTS], U8)
+        hid = sbuf("hid", [P, PACK * PLACES], BF16)
+
+        def tower(name, i, lhs, got, got_s, fmt):
+            acc = psum.tile([P, SLOTS], F32, name="acc_" + name)
+            nc.tensor.matmul_mx(
+                out=acc[:], lhsT=lhs, lhsT_scale=w_plane[:, FEATS * i : FEATS * (i + 1)],
+                rhs=got[:].bitcast(fmt), rhs_scale=got_s[:], start=True, stop=True,
+            )
+            return acc
+
+        def fetch(res, lst, name, t):
+            nc.scalar.activation(
+                out=hid[:, t : PACK * PLACES : PACK], in_=res[:].indirect(lst[:]), func=COPY, scale=factors[name][:]
+            )
+
+        spread(xt_plane, xt_stage)
+        nc.vector.tensor_copy(xt_got[:], xt_tab[:].bitcast(U32).indirect(l_xt[:]))
+        nc.vector.tensor_copy(xt_got_s[:], xt_plane[:].indirect(l_xt[:]))
+        spread(w_plane, w_stage)
+        acc_a = tower("a", 0, w_sb[:].bitcast(E2M1), xt_got, xt_got_s, E5M2)
+        acc_b = tower("b", 1, w2_sb[:].bitcast(E2M1), xt_got, xt_got_s, E5M2)
+        spread(xo_plane, xo_stage)
+        nc.vector.tensor_copy(xo_got[:], xo_tab[:].bitcast(U32).indirect(l_xo[:]))
+        nc.vector.tensor_copy(xo_got_s[:], xo_plane[:].indirect(l_xo[:]))
+        acc_g = tower("g", 2, w3_sb[:].bitcast(E4M3), xo_got, xo_got_s, E4M3)
+        acc_d = tower("d", 3, w0_sb[:].bitcast(E2M1), xo_got, xo_got_s, E4M3)
+
+        res_a = sbuf("res_a", [P, SLOTS], F32)
+        res_b = sbuf("res_b", [P, SLOTS], F32)
+        res_g = sbuf("res_g", [P, SLOTS], F32)
+        res_d = sbuf("res_d", [P, SLOTS], F32)
+        nc.scalar.activation(out=res_a[:], in_=acc_a[:], func=COPY)
+        nc.scalar.activation(out=res_b[:], in_=acc_b[:], func=COPY)
+        fetch(res_a, l_a, "a", 0)
+        fetch(res_b, l_b, "b", 2)
+        nc.vector.tensor_copy(res_g[:], acc_g[:])
+        nc.vector.tensor_copy(res_d[:], acc_d[:])
+        fetch(res_g, l_g, "g", 1)
+        fetch(res_d, l_d, "d", 3)
+
+        hid_codes = sbuf("hid_codes", [P, PLACES], U32)
+        hid_plane = sbuf("hid_plane", [P, PLACES], U8)
+        nc.vector.quantize_mx(out=hid_codes[:].bitcast(E4M3), scales=hid_plane[:], in_=hid[:])
+
+        for h in range(OUTS // P):
+            acc = psum.tile([P, PLACES], F32, name="acc_out%d" % h)
+            nc.tensor.matmul_mx(
+                out=acc[:], lhsT=wb_sb[:, 2 * P * h : 2 * P * (h + 1)].bitcast(E2M1),
+                lhsT_scale=wb_plane[:, P * h : P * (h + 1)],
+                rhs=hid_codes[:].bitcast(E4M3), rhs_scale=hid_plane[:], start=True, stop=True,
+            )
+            res = sbuf("res_out%d" % h, [P, PLACES], F32)
+            if h == 0:
+                nc.vector.tensor_copy(res[:], acc[:])
+                nc.sync.dma_start(out[P * h : P * (h + 1), :], res[:])
+            else:
+                nc.scalar.copy(res[:], acc[:])
+                nc.scalar.dma_start(out[P * h : P * (h + 1), :], res[:])

@@ -36,8 +36,8 @@ def tile_list_fourtowers_kernel(
         pool = ctx.enter_context(tc.tile_pool(name="held", bufs=1))
         psum = ctx.enter_context(tc.psum_pool(name="psum", bufs=1))
 
-        def sbuf(name, shape, dtype):
-            return pool.tile(shape, dtype, name=name, align_bytes=64)
+        def sbuf(name, shape, dtype, tag=None):
+            return pool.tile(shape, dtype, name=name, tag=tag or name, align_bytes=64)
 
         def list_tile(name, src):
             tile = sbuf(name, list(src.shape), U16)
@@ -50,121 +50,114 @@ def tile_list_fourtowers_kernel(
         def by_quadrant(src):
             return src[0].bitcast(I32).rearrange("(q r) n -> r q n", r=ROWS)
 
-        def spread(plane, stage):
-            for q in range(QUADS):
+        def spread(plane, stage, n, first=0):
+            for q in range(first, n):
                 nc.vector.tensor_copy(plane[32 * q : 32 * q + ROWS, :].bitcast(I32), stage[0:ROWS, q, :])
 
+        def direct(queue, plane, src, q):
+            queue.dma_start(plane[q:P:32, :].bitcast(I32), src[0, q:16:ROWS, :].bitcast(I32))
+
         xt_tab = sbuf("xt_tab", [P, COLS], I32)
-        xo_tab = sbuf("xo_tab", [P, COLS], I32)
-        xt_stage = sbuf("xt_stage", [ROWS, QUADS, COLS // 4], I32)
-        xo_stage = sbuf("xo_stage", [ROWS, QUADS, COLS // 4], I32)
         xt_plane = sbuf("xt_plane", [P, COLS], U8)
+        xt_stage = sbuf("xt_stage", [ROWS, 4, COLS // 4], I32)
+        xo_tab = sbuf("xo_tab", [P, COLS], I32)
         xo_plane = sbuf("xo_plane", [P, COLS], U8)
-        w_stage = sbuf("w_stage", [ROWS, QUADS, FEATS], I32)
-        w_plane = sbuf("w_plane", [P, 4 * FEATS], U8)
-        wb_plane = sbuf("wb_plane", [P, OUTS], U8)
-        w_sb = sbuf("w_sb", [P, 2 * FEATS], U8)
-        w2_sb = sbuf("w2_sb", [P, 2 * FEATS], U8)
-        w3_sb = sbuf("w3_sb", [P, FEATS], I32)
-        w0_sb = sbuf("w0_sb", [P, 2 * FEATS], U8)
-        wb_sb = sbuf("wb_sb", [P, 2 * OUTS], U8)
-
-        for plane in (xt_plane, xo_plane, w_plane, wb_plane):
-            nc.vector.memset(plane[:].bitcast(I32), 0)
-
-        def stage_w(i, src):
-            nc.scalar.dma_start(w_stage[:, :, 32 * i : 32 * (i + 1)], by_quadrant(src))
-
-        nc.sync.dma_start(xt_tab[:], fp8_words(xt_words))
-        nc.scalar.dma_start(xt_stage[:], by_quadrant(xt_scales))
-        l_xt = list_tile("l_xt", offs)
-        nc.scalar.dma_start(xo_stage[:], by_quadrant(xo_scales))
-        nc.sync.dma_start(xo_tab[:], fp8_words(xo_words))
-        stage_w(0, w_scales)
-        l_xo = list_tile("l_xo", offs2)
-        stage_w(1, w2_scales)
-
+        xo_stage = sbuf("xo_stage", [ROWS, 4, COLS // 4], I32)
+        w_rows0 = sbuf("w_rows0", [P, QUADS * 512], U8)
+        w_plane0 = w_rows0[:, 0:512]
+        w_stage0 = w_rows0[:].bitcast(I32).rearrange("p (q n) -> p q n", q=QUADS)[0:ROWS]
+        wb_rows = sbuf("wb_rows", [P, QUADS * OUTS], U8)
+        wb_plane = wb_rows[:, 0:OUTS]
+        wb_stage = wb_rows[:].bitcast(I32).rearrange("p (q n) -> p q n", q=QUADS)[0:ROWS]
+        w_a = sbuf("w_a", [P, 256], U8)
+        w_b = sbuf("w_b", [P, 256], U8)
+        w_d = sbuf("w_d", [P, 256], U8)
+        w_wb = sbuf("w_wb", [P, 512], U8)
+        w_g = sbuf("w_g", [P, FEATS], I32)
         factors = {}
-        for name, src in (("a", sa), ("b", sb), ("g", sd), ("d", se)):
+        for name in "abgd":
             factors[name] = sbuf("f_" + name, [P, 1], F32)
-            nc.gpsimd.dma_start(factors[name][:], src)
-        nc.gpsimd.dma_start(wb_sb[:].bitcast(I32), wb_words[0].bitcast(I32))
-
-        nc.scalar.dma_start(w_sb[:].bitcast(I32), w_words[0].bitcast(I32))
-        nc.sync.dma_start(w3_sb[:], fp8_words(w3_words))
-        nc.scalar.dma_start(w2_sb[:].bitcast(I32), w2_words[0].bitcast(I32))
-        nc.sync.dma_start(w0_sb[:].bitcast(I32), w0_words[0].bitcast(I32))
-        stage_w(2, w3_scales)
+        nc.vector.memset(w_plane0[:].bitcast(I32), 0)
+        nc.vector.memset(xt_plane[:].bitcast(I32), 0)
+        nc.vector.memset(xo_plane[:].bitcast(I32), 0)
+        nc.vector.memset(wb_plane[:].bitcast(I32), 0)
+        l_xt = list_tile("l_xt", offs)
+        nc.scalar.dma_start(xt_stage[:], by_quadrant(xt_scales)[:, 0:4, :])
+        nc.sync.dma_start(w_a[:].bitcast(I32), w_words[0].bitcast(I32))
+        nc.sync.dma_start(xt_tab[:], fp8_words(xt_words))
+        nc.scalar.dma_start(xo_stage[:], by_quadrant(xo_scales)[:, 0:4, :])
+        nc.sync.dma_start(xo_tab[:], fp8_words(xo_words))
+        nc.scalar.dma_start(w_stage0[:, :, 0:32], by_quadrant(w_scales))
+        nc.scalar.dma_start(w_stage0[:, :, 32:64], by_quadrant(w2_scales))
+        nc.sync.dma_start(w_stage0[:, :, 96:128], by_quadrant(w0_scales))
+        nc.scalar.dma_start(w_stage0[:, :, 64:96], by_quadrant(w3_scales))
+        l_xo = list_tile("l_xo", offs2)
+        nc.scalar.dma_start(w_b[:].bitcast(I32), w2_words[0].bitcast(I32))
         l_a = list_tile("l_a", offs3)
-        stage_w(3, w0_scales)
+        nc.sync.dma_start(factors["a"][:], sa)
+        nc.sync.dma_start(w_d[:].bitcast(I32), w0_words[0].bitcast(I32))
         l_b = list_tile("l_b", offs5)
+        nc.sync.dma_start(factors["b"][:], sb)
         l_g = list_tile("l_g", offs4)
+        nc.sync.dma_start(factors["g"][:], sd)
+        nc.sync.dma_start(wb_stage[:], by_quadrant(wb_scales))
         l_d = list_tile("l_d", offs6)
-        for q in range(QUADS):
-            nc.sync.dma_start(
-                wb_plane[32 * q : 32 * q + ROWS, :].bitcast(I32),
-                wb_scales[0, ROWS * q : ROWS * (q + 1), :].bitcast(I32),
-            )
-
+        nc.gpsimd.dma_start(w_g[:], fp8_words(w3_words))
+        nc.gpsimd.dma_start(factors["d"][:], se)
+        nc.gpsimd.dma_start(w_wb[:].bitcast(I32), wb_words[0].bitcast(I32))
         xt_got = sbuf("xt_got", [P, SLOTS], U32)
         xo_got = sbuf("xo_got", [P, SLOTS], U32)
         xt_got_s = sbuf("xt_got_s", [P, SLOTS], U8)
         xo_got_s = sbuf("xo_got_s", [P, SLOTS], U8)
         hid = sbuf("hid", [P, PACK * PLACES], BF16)
-
-        def tower(name, i, lhs, got, got_s, fmt):
-            acc = psum.tile([P, SLOTS], F32, name="acc_" + name)
-            nc.tensor.matmul_mx(
-                out=acc[:], lhsT=lhs, lhsT_scale=w_plane[:, FEATS * i : FEATS * (i + 1)],
-                rhs=got[:].bitcast(fmt), rhs_scale=got_s[:], start=True, stop=True,
-            )
-            return acc
-
-        def fetch(res, lst, name, t):
-            nc.scalar.activation(
-                out=hid[:, t : PACK * PLACES : PACK], in_=res[:].indirect(lst[:]), func=COPY, scale=factors[name][:]
-            )
-
-        spread(xt_plane, xt_stage)
-        nc.vector.tensor_copy(xt_got[:], xt_tab[:].bitcast(U32).indirect(l_xt[:]))
+        acc = {}
+        res = {}
+        for name in "abgd":
+            if name in "g":
+                for h in "01":
+                    acc[name + h] = psum.tile([P, SLOTS // 2], F32, name="acc_" + name + h)
+            else:
+                acc[name] = psum.tile([P, SLOTS], F32, name="acc_" + name)
+            res[name] = sbuf("res_" + name, [P, SLOTS], F32)
+        spread(xt_plane, xt_stage, 4)
         nc.vector.tensor_copy(xt_got_s[:], xt_plane[:].indirect(l_xt[:]))
-        spread(w_plane, w_stage)
-        acc_a = tower("a", 0, w_sb[:].bitcast(E2M1), xt_got, xt_got_s, E5M2)
-        acc_b = tower("b", 1, w2_sb[:].bitcast(E2M1), xt_got, xt_got_s, E5M2)
-        spread(xo_plane, xo_stage)
-        nc.vector.tensor_copy(xo_got[:], xo_tab[:].bitcast(U32).indirect(l_xo[:]))
+        nc.vector.tensor_copy(xt_got[:], xt_tab[:].bitcast(U32).indirect(l_xt[:]))
+        spread(xo_plane, xo_stage, 4)
+        spread(w_plane0, w_stage0, QUADS, 1)
+        nc.tensor.matmul_mx(out=acc["a"][:], lhsT=w_a[:].bitcast(E2M1), lhsT_scale=w_plane0[:, 0:128], rhs=xt_got[:].bitcast(E5M2), rhs_scale=xt_got_s[:], start=True, stop=True)
+        nc.tensor.matmul_mx(out=acc["b"][:], lhsT=w_b[:].bitcast(E2M1), lhsT_scale=w_plane0[:, 128:256], rhs=xt_got[:].bitcast(E5M2), rhs_scale=xt_got_s[:], start=True, stop=True)
         nc.vector.tensor_copy(xo_got_s[:], xo_plane[:].indirect(l_xo[:]))
-        acc_g = tower("g", 2, w3_sb[:].bitcast(E4M3), xo_got, xo_got_s, E4M3)
-        acc_d = tower("d", 3, w0_sb[:].bitcast(E2M1), xo_got, xo_got_s, E4M3)
-
-        res_a = sbuf("res_a", [P, SLOTS], F32)
-        res_b = sbuf("res_b", [P, SLOTS], F32)
-        res_g = sbuf("res_g", [P, SLOTS], F32)
-        res_d = sbuf("res_d", [P, SLOTS], F32)
-        nc.scalar.activation(out=res_a[:], in_=acc_a[:], func=COPY)
-        nc.scalar.activation(out=res_b[:], in_=acc_b[:], func=COPY)
-        fetch(res_a, l_a, "a", 0)
-        fetch(res_b, l_b, "b", 2)
-        nc.vector.tensor_copy(res_g[:], acc_g[:])
-        nc.vector.tensor_copy(res_d[:], acc_d[:])
-        fetch(res_g, l_g, "g", 1)
-        fetch(res_d, l_d, "d", 3)
+        nc.vector.tensor_copy(xo_got[:, 0:128], xo_tab[:].bitcast(U32).indirect(l_xo[:, 0:8]))
+        nc.tensor.matmul_mx(out=acc["g0"][:], lhsT=w_g[:].bitcast(E4M3), lhsT_scale=w_plane0[:, 256:384], rhs=xo_got[:, 0:128].bitcast(E4M3), rhs_scale=xo_got_s[:, 0:128], start=True, stop=True)
+        nc.vector.tensor_copy(xo_got[:, 128:256], xo_tab[:].bitcast(U32).indirect(l_xo[:, 8:16]))
+        nc.tensor.matmul_mx(out=acc["g1"][:], lhsT=w_g[:].bitcast(E4M3), lhsT_scale=w_plane0[:, 256:384], rhs=xo_got[:, 128:256].bitcast(E4M3), rhs_scale=xo_got_s[:, 128:256], start=True, stop=True)
+        nc.tensor.matmul_mx(out=acc["d"][:], lhsT=w_d[:].bitcast(E2M1), lhsT_scale=w_plane0[:, 384:512], rhs=xo_got[:].bitcast(E4M3), rhs_scale=xo_got_s[:], start=True, stop=True)
+        nc.scalar.activation(out=res["a"][:], in_=acc["a"][:], func=COPY)
+        nc.scalar.activation(out=hid[:, 0 : PACK * PLACES : PACK], in_=res["a"][:].indirect(l_a[:]), func=COPY, scale=factors["a"][:])
+        nc.vector.tensor_copy(res["g"][:, 0:128], acc["g0"][:])
+        nc.vector.tensor_copy(res["g"][:, 128:256], acc["g1"][:])
+        nc.vector.tensor_copy(res["b"][:], acc["b"][:])
+        nc.scalar.activation(out=hid[:, 2 : PACK * PLACES : PACK], in_=res["b"][:].indirect(l_b[:]), func=COPY, scale=factors["b"][:])
+        nc.vector.tensor_copy(res["d"][:], acc["d"][:])
+        spread(wb_plane, wb_stage, QUADS, 1)
+        nc.scalar.activation(out=hid[:, 1 : PACK * PLACES : PACK], in_=res["g"][:].indirect(l_g[:]), func=COPY, scale=factors["g"][:])
+        nc.scalar.activation(out=hid[:, 3 : PACK * PLACES : PACK], in_=res["d"][:].indirect(l_d[:]), func=COPY, scale=factors["d"][:])
 
         hid_codes = sbuf("hid_codes", [P, PLACES], U32)
         hid_plane = sbuf("hid_plane", [P, PLACES], U8)
         nc.vector.quantize_mx(out=hid_codes[:].bitcast(E4M3), scales=hid_plane[:], in_=hid[:])
 
         for h in range(OUTS // P):
-            acc = psum.tile([P, PLACES], F32, name="acc_out%d" % h)
+            acc_o = psum.tile([P, PLACES], F32, name="acc_out%d" % h)
             nc.tensor.matmul_mx(
-                out=acc[:], lhsT=wb_sb[:, 2 * P * h : 2 * P * (h + 1)].bitcast(E2M1),
+                out=acc_o[:], lhsT=w_wb[:, 2 * P * h : 2 * P * (h + 1)].bitcast(E2M1),
                 lhsT_scale=wb_plane[:, P * h : P * (h + 1)],
                 rhs=hid_codes[:].bitcast(E4M3), rhs_scale=hid_plane[:], start=True, stop=True,
             )
-            res = sbuf("res_out%d" % h, [P, PLACES], F32)
+            res_o = sbuf("res_out%d" % h, [P, PLACES], F32)
             if h == 0:
-                nc.vector.tensor_copy(res[:], acc[:])
-                nc.sync.dma_start(out[P * h : P * (h + 1), :], res[:])
+                nc.vector.tensor_copy(res_o[:], acc_o[:])
+                nc.sync.dma_start(out[P * h : P * (h + 1), :], res_o[:])
             else:
-                nc.scalar.copy(res[:], acc[:])
-                nc.scalar.dma_start(out[P * h : P * (h + 1), :], res[:])
+                nc.scalar.copy(res_o[:], acc_o[:])
+                nc.scalar.dma_start(out[P * h : P * (h + 1), :], res_o[:])

from contextlib import ExitStack

import concourse.mybir as mybir

F32 = mybir.dt.float32
BF16 = mybir.dt.bfloat16
I32 = mybir.dt.int32
U32 = mybir.dt.uint32
U16 = mybir.dt.uint16
U8 = mybir.dt.uint8
E4M3 = mybir.dt.float8_e4m3fn_x4
E5M2 = mybir.dt.float8_e5m2_x4
E2M1 = mybir.dt.float4_e2m1fn_x4
COPY = mybir.ActivationFunctionType.Copy

P = 128
COLS = 1024
SLOTS = 256
FEATS = 128
PLACES = 128
OUTS = 256
QUADS = 4
ROWS = 4
PACK = 4

FLOPS = 2 * 512 * FEATS * SLOTS * 4 + 2 * 512 * OUTS * PLACES


def tile_list_fourtowers_kernel(
    tc, xt_words, xt_scales, xo_words, xo_scales, w_words, w_scales, w2_words, w2_scales,
    w3_words, w3_scales, w0_words, w0_scales, sa, sb, sd, se, wb_words, wb_scales,
    offs, offs2, offs3, offs4, offs5, offs6, out,
):
    nc = tc.nc
    with ExitStack() as ctx:
        pool = ctx.enter_context(tc.tile_pool(name="held", bufs=1))
        psum = ctx.enter_context(tc.psum_pool(name="psum", bufs=1))

        def sbuf(name, shape, dtype, tag=None):
            return pool.tile(shape, dtype, name=name, tag=tag or name, align_bytes=64)

        def list_tile(name, src):
            tile = sbuf(name, list(src.shape), U16)
            nc.sync.dma_start(tile[:], src)
            return tile

        def fp8_words(src):
            return src[0].rearrange("p c r -> p (c r)").bitcast(I32)

        def by_quadrant(src):
            return src[0].bitcast(I32).rearrange("(q r) n -> r q n", r=ROWS)

        def spread(plane, stage, n, first=0):
            for q in range(first, n):
                nc.vector.tensor_copy(plane[32 * q : 32 * q + ROWS, :].bitcast(I32), stage[0:ROWS, q, :])

        def direct(queue, plane, src, q):
            queue.dma_start(plane[q:P:32, :].bitcast(I32), src[0, q:16:ROWS, :].bitcast(I32))

        xt_tab = sbuf("xt_tab", [P, COLS], I32)
        xt_plane = sbuf("xt_plane", [P, COLS], U8)
        xt_stage = sbuf("xt_stage", [ROWS, 4, COLS // 4], I32)
        xo_tab = sbuf("xo_tab", [P, COLS], I32)
        xo_plane = sbuf("xo_plane", [P, COLS], U8)
        xo_stage = sbuf("xo_stage", [ROWS, 4, COLS // 4], I32)
        w_rows0 = sbuf("w_rows0", [P, QUADS * 512], U8)
        w_plane0 = w_rows0[:, 0:512]
        w_stage0 = w_rows0[:].bitcast(I32).rearrange("p (q n) -> p q n", q=QUADS)[0:ROWS]
        wb_rows = sbuf("wb_rows", [P, QUADS * OUTS], U8)
        wb_plane = wb_rows[:, 0:OUTS]
        wb_stage = wb_rows[:].bitcast(I32).rearrange("p (q n) -> p q n", q=QUADS)[0:ROWS]
        w_a = sbuf("w_a", [P, 256], U8)
        w_b = sbuf("w_b", [P, 256], U8)
        w_d = sbuf("w_d", [P, 256], U8)
        w_wb = sbuf("w_wb", [P, 512], U8)
        w_g = sbuf("w_g", [P, FEATS], I32)
        factors = {}
        for name in "abgd":
            factors[name] = sbuf("f_" + name, [P, 1], F32)
        nc.vector.memset(w_plane0[:].bitcast(I32), 0)
        nc.vector.memset(xt_plane[:].bitcast(I32), 0)
        nc.vector.memset(xo_plane[:].bitcast(I32), 0)
        nc.vector.memset(wb_plane[:].bitcast(I32), 0)
        l_xt = list_tile("l_xt", offs)
        nc.scalar.dma_start(xt_stage[:], by_quadrant(xt_scales)[:, 0:4, :])
        nc.sync.dma_start(w_a[:].bitcast(I32), w_words[0].bitcast(I32))
        nc.sync.dma_start(xt_tab[:], fp8_words(xt_words))
        nc.scalar.dma_start(xo_stage[:], by_quadrant(xo_scales)[:, 0:4, :])
        nc.sync.dma_start(xo_tab[:], fp8_words(xo_words))
        nc.scalar.dma_start(w_stage0[:, :, 0:32], by_quadrant(w_scales))
        nc.scalar.dma_start(w_stage0[:, :, 32:64], by_quadrant(w2_scales))
        nc.sync.dma_start(w_stage0[:, :, 96:128], by_quadrant(w0_scales))
        nc.scalar.dma_start(w_stage0[:, :, 64:96], by_quadrant(w3_scales))
        l_xo = list_tile("l_xo", offs2)
        nc.scalar.dma_start(w_b[:].bitcast(I32), w2_words[0].bitcast(I32))
        l_a = list_tile("l_a", offs3)
        nc.sync.dma_start(factors["a"][:], sa)
        nc.sync.dma_start(w_d[:].bitcast(I32), w0_words[0].bitcast(I32))
        l_b = list_tile("l_b", offs5)
        nc.sync.dma_start(factors["b"][:], sb)
        l_g = list_tile("l_g", offs4)
        nc.sync.dma_start(factors["g"][:], sd)
        nc.sync.dma_start(wb_stage[:], by_quadrant(wb_scales))
        l_d = list_tile("l_d", offs6)
        nc.gpsimd.dma_start(w_g[:], fp8_words(w3_words))
        nc.gpsimd.dma_start(factors["d"][:], se)
        nc.gpsimd.dma_start(w_wb[:].bitcast(I32), wb_words[0].bitcast(I32))
        xt_got = sbuf("xt_got", [P, SLOTS], U32)
        xo_got = sbuf("xo_got", [P, SLOTS], U32)
        xt_got_s = sbuf("xt_got_s", [P, SLOTS], U8)
        xo_got_s = sbuf("xo_got_s", [P, SLOTS], U8)
        hid = sbuf("hid", [P, PACK * PLACES], BF16)
        acc = {}
        res = {}
        for name in "abgd":
            if name in "g":
                for h in "01":
                    acc[name + h] = psum.tile([P, SLOTS // 2], F32, name="acc_" + name + h)
            else:
                acc[name] = psum.tile([P, SLOTS], F32, name="acc_" + name)
            res[name] = sbuf("res_" + name, [P, SLOTS], F32)
        spread(xt_plane, xt_stage, 4)
        nc.vector.tensor_copy(xt_got_s[:], xt_plane[:].indirect(l_xt[:]))
        nc.vector.tensor_copy(xt_got[:], xt_tab[:].bitcast(U32).indirect(l_xt[:]))
        spread(xo_plane, xo_stage, 4)
        spread(w_plane0, w_stage0, QUADS, 1)
        nc.tensor.matmul_mx(out=acc["a"][:], lhsT=w_a[:].bitcast(E2M1), lhsT_scale=w_plane0[:, 0:128], rhs=xt_got[:].bitcast(E5M2), rhs_scale=xt_got_s[:], start=True, stop=True)
        nc.tensor.matmul_mx(out=acc["b"][:], lhsT=w_b[:].bitcast(E2M1), lhsT_scale=w_plane0[:, 128:256], rhs=xt_got[:].bitcast(E5M2), rhs_scale=xt_got_s[:], start=True, stop=True)
        nc.vector.tensor_copy(xo_got_s[:], xo_plane[:].indirect(l_xo[:]))
        nc.vector.tensor_copy(xo_got[:, 0:128], xo_tab[:].bitcast(U32).indirect(l_xo[:, 0:8]))
        nc.tensor.matmul_mx(out=acc["g0"][:], lhsT=w_g[:].bitcast(E4M3), lhsT_scale=w_plane0[:, 256:384], rhs=xo_got[:, 0:128].bitcast(E4M3), rhs_scale=xo_got_s[:, 0:128], start=True, stop=True)
        nc.vector.tensor_copy(xo_got[:, 128:256], xo_tab[:].bitcast(U32).indirect(l_xo[:, 8:16]))
        nc.tensor.matmul_mx(out=acc["g1"][:], lhsT=w_g[:].bitcast(E4M3), lhsT_scale=w_plane0[:, 256:384], rhs=xo_got[:, 128:256].bitcast(E4M3), rhs_scale=xo_got_s[:, 128:256], start=True, stop=True)
        nc.tensor.matmul_mx(out=acc["d"][:], lhsT=w_d[:].bitcast(E2M1), lhsT_scale=w_plane0[:, 384:512], rhs=xo_got[:].bitcast(E4M3), rhs_scale=xo_got_s[:], start=True, stop=True)
        nc.scalar.activation(out=res["a"][:], in_=acc["a"][:], func=COPY)
        nc.scalar.activation(out=hid[:, 0 : PACK * PLACES : PACK], in_=res["a"][:].indirect(l_a[:]), func=COPY, scale=factors["a"][:])
        nc.vector.tensor_copy(res["g"][:, 0:128], acc["g0"][:])
        nc.vector.tensor_copy(res["g"][:, 128:256], acc["g1"][:])
        nc.vector.tensor_copy(res["b"][:], acc["b"][:])
        nc.scalar.activation(out=hid[:, 2 : PACK * PLACES : PACK], in_=res["b"][:].indirect(l_b[:]), func=COPY, scale=factors["b"][:])
        nc.vector.tensor_copy(res["d"][:], acc["d"][:])
        spread(wb_plane, wb_stage, QUADS, 1)
        nc.scalar.activation(out=hid[:, 1 : PACK * PLACES : PACK], in_=res["g"][:].indirect(l_g[:]), func=COPY, scale=factors["g"][:])
        nc.scalar.activation(out=hid[:, 3 : PACK * PLACES : PACK], in_=res["d"][:].indirect(l_d[:]), func=COPY, scale=factors["d"][:])

        hid_codes = sbuf("hid_codes", [P, PLACES], U32)
        hid_plane = sbuf("hid_plane", [P, PLACES], U8)
        nc.vector.quantize_mx(out=hid_codes[:].bitcast(E4M3), scales=hid_plane[:], in_=hid[:])

        for h in range(OUTS // P):
            acc_o = psum.tile([P, PLACES], F32, name="acc_out%d" % h)
            nc.tensor.matmul_mx(
                out=acc_o[:], lhsT=w_wb[:, 2 * P * h : 2 * P * (h + 1)].bitcast(E2M1),
                lhsT_scale=wb_plane[:, P * h : P * (h + 1)],
                rhs=hid_codes[:].bitcast(E4M3), rhs_scale=hid_plane[:], start=True, stop=True,
            )
            res_o = sbuf("res_out%d" % h, [P, PLACES], F32)
            if h == 0:
                nc.vector.tensor_copy(res_o[:], acc_o[:])
                nc.sync.dma_start(out[P * h : P * (h + 1), :], res_o[:])
            else:
                nc.scalar.copy(res_o[:], acc_o[:])
                nc.scalar.dma_start(out[P * h : P * (h + 1), :], res_o[:])
